import numpy as np
import ml_dtypes


def mxq(x, axis, fmt="e4m3"):
    dtype, down = {"e4m3": (ml_dtypes.float8_e4m3fn, 7), "e5m2": (ml_dtypes.float8_e5m2, 14)}[fmt]
    v = np.moveaxis(np.asarray(x, np.float32).astype(ml_dtypes.bfloat16).astype(np.float64), axis, -1)
    blocks = v.reshape(v.shape[:-1] + (-1, 32))
    amax = np.abs(blocks).max(-1, keepdims=True)
    byte = np.maximum(np.where(amax > 0, np.frexp(amax)[1] - 1 + 127, 0) - down, 1)
    scale = np.exp2(byte - 127.0)
    codes = (blocks / scale).astype(np.float32).astype(dtype).astype(np.float64)
    return np.moveaxis((codes * scale).reshape(v.shape), -1, axis)


WIDE = False


def mx_kscale(k):
    if not WIDE:
        return np.ones(k)
    levels = np.array([10, -10, 5, -5, 0])
    if k % 512:
        return np.exp2(np.random.permutation(np.resize(levels, k // 32))).repeat(32)
    a = np.empty((k // 512, 16))
    for p in range(k // 512):
        a[p, :8] = np.random.permutation(np.resize(levels, 8))
        for g in range(8):
            far = levels[np.abs(levels - a[p, g]) >= 10]
            a[p, g + 8] = far[np.random.randint(len(far))]
    return np.exp2(a.ravel()).repeat(32)


def f64(x):
    return np.asarray(x).astype(np.float64)


def striped(idx):
    return np.tile(idx.reshape(-1, 16).T, (8, 1)).astype(np.uint16)


def unstriped(offs):
    return offs[:16].T.reshape(-1).astype(np.int64)


def striped8(idx):
    return np.concatenate([x.reshape(-1, 16).T for x in idx]).astype(np.uint16)


def runs(offs, k):
    lists = np.stack([offs[16 * r : 16 * r + 16].T.reshape(-1) for r in range(8)]).astype(np.int64)
    return lists[np.arange(k) % 512 // 64]


def pack_weight(w):
    k, n = w.shape
    w = f64(np.asarray(w, np.float32).astype(ml_dtypes.bfloat16)).reshape(k // 32, 32, n)
    amax = np.abs(w).max(1)
    byte = np.clip(np.where(amax > 0, np.frexp(amax)[1] - 1 + 127 - 7, 1), 1, 254)
    scaled = (w * np.exp2(127.0 - byte)[:, None, :]).reshape(k, n).astype(np.float32)
    words = np.ascontiguousarray(scaled.reshape(k // 512, 128, 4, n).transpose(0, 1, 3, 2)).astype(ml_dtypes.float8_e4m3fn).view(np.uint8)
    return words, np.ascontiguousarray(byte.astype(np.uint8).reshape(k // 512, 16, n))


def unpack_weight(words, scales):
    g, p, n, _ = words.shape
    vals = np.ascontiguousarray(words).view(ml_dtypes.float8_e4m3fn).astype(np.float64) * np.repeat(np.exp2(scales.astype(np.float64) - 127.0), 8, axis=1)[..., None]
    return vals.transpose(0, 1, 3, 2).reshape(g * 512, n)

def planes(y):
    n, m = y.shape
    v = y.astype(np.float32).astype(ml_dtypes.bfloat16).astype(np.float64).reshape(n // 32, 32, m)
    top = np.abs(v).max(1)
    byte = np.clip(np.where(top > 0, np.frexp(top)[1] - 1 + 127 - 7, 1), 1, 254)
    codes = (v * np.exp2(127.0 - byte)[:, None, :]).reshape(n, m).astype(np.float32).astype(ml_dtypes.float8_e4m3fn).view(np.uint8)
    words = codes.reshape(n // 512, 128, 4, m).transpose(0, 1, 3, 2)
    return np.ascontiguousarray(words), np.ascontiguousarray(byte.astype(np.uint8).reshape(n // 512, 16, m))


K, T, S, V, N, H, U = 512, 2048, 1024, 512, 512, 512, 1024


def setup_inputs():
    n = np.random.standard_normal
    s = mx_kscale(K)[:, None]
    u = mx_kscale(H)
    packed_xT = pack_weight(n((K, T)) * s)
    packed_w1 = pack_weight(n((K, H)) / np.sqrt(K) / s)
    packed_w2 = pack_weight(n((H, N)) / np.sqrt(H) / u[:, None])
    return {
        "x_words": packed_xT[0],
        "x_scales": packed_xT[1],
        "w1_words": packed_w1[0],
        "w1_scales": packed_w1[1],
        "gn": (np.random.uniform(0.5, 1.5, (H, 1)) * u[:, None]).astype(np.float32),
        "w2_words": packed_w2[0],
        "w2_scales": packed_w2[1],
        "mem": n((N, U)).astype(np.float32),
        "offs": striped(np.random.permutation(T)[:S]),
        "n1": striped8(np.stack([np.random.permutation(S) for _ in range(8)])),
        "n2": striped8(np.stack([np.random.permutation(U)[:V] for _ in range(8)])),
        "n3": striped8(np.stack([np.random.permutation(U) for _ in range(8)])),
    }


def reference(x_words, x_scales, w1_words, w1_scales, gn, w2_words, w2_scales, mem, offs, n1, n2, n3):
    xq = unpack_weight(x_words, x_scales)[:, unstriped(offs)]
    y = unpack_weight(w1_words, w1_scales).T @ xq
    ln = y[np.arange(H)[:, None], runs(n1, H)]
    mx = ln.reshape(H, V, 2).max(axis=2)
    mn = ln.reshape(H, V, 2).min(axis=2)
    z = f64(gn) * (mx - (0.5 * mn))
    h = unpack_weight(w2_words, w2_scales).T @ mxq(z, 0, "e4m3")
    pg = f64(mem).copy()
    pg[np.arange(N)[:, None], runs(n2, N)] = h
    out_0 = pg - (0.5 * (pg[np.arange(N)[:, None], runs(n3, N)]))
    return (out_0,) + planes(out_0)

@@ -1,0 +1,238 @@
+from contextlib import ExitStack
+
+import concourse.mybir as mybir
+
+K, T, S, V, N, H, U = 512, 2048, 1024, 512, 512, 512, 1024
+FLOPS = 2 * K * H * S + 2 * H * N * V
+
+F32 = mybir.dt.float32
+BF16 = mybir.dt.bfloat16
+I32 = mybir.dt.int32
+U32 = mybir.dt.uint32
+U16 = mybir.dt.uint16
+U8 = mybir.dt.uint8
+FP8X4 = mybir.dt.float8_e4m3fn_x4
+ALU = mybir.AluOpType
+COPY = mybir.ActivationFunctionType.Copy
+
+P = 128
+PACK = 4
+LANES = 16
+HALF = S // 2
+PAIRS = HALF // 2
+OUT_CHUNK = 256
+
+
+def tile_picked_laypgappagem_none_po_kernel(
+    tc, x_words, x_scales, w1_words, w1_scales, gn, w2_words, w2_scales, mem, offs, n1, n2, n3, out_0, out_1, out_2
+):
+    nc = tc.nc
+
+    def as_words(words):
+        return words[0].rearrange("p c r -> p (c r)").bitcast(I32)
+
+    def load_scale_rows(plane, scales):
+        for q in range(4):
+            nc.sync.dma_start(out=plane[32 * q : 32 * q + 4, :].bitcast(I32), in_=scales[0, 4 * q : 4 * q + 4, :].bitcast(I32))
+
+    def deal(dealt, raw):
+        nc.vector.tensor_copy(
+            out=dealt[:].rearrange("p (t m) -> p m t", t=PACK), in_=raw[:].rearrange("p (m t) -> p m t", t=PACK)
+        )
+
+    def entries(list_tile, first, count):
+        return list_tile[:, first // LANES : (first + count) // LANES]
+
+    with ExitStack() as ctx:
+        lists = ctx.enter_context(tc.tile_pool(name="lists", bufs=1))
+        keep = ctx.enter_context(tc.tile_pool(name="keep", bufs=1))
+        psum = ctx.enter_context(tc.psum_pool(name="psum", bufs=8))
+
+        offs_t = lists.tile([P, S // LANES], U16, name="offs_t")
+        n1_t = lists.tile([P, S // LANES], U16, name="n1_t")
+        n2_t = lists.tile([P, V // LANES], U16, name="n2_t")
+        n3_t = lists.tile([P, U // LANES], U16, name="n3_t")
+
+        xs_all = keep.tile([P, T], U8, name="xs_all", align_bytes=64)
+        xw_all = keep.tile([P, T], I32, name="xw_all", align_bytes=64)
+        w1s_raw = keep.tile([P, H], U8, name="w1s_raw", tag="w1s_raw", align_bytes=64)
+        w1w_raw = keep.tile([P, H], I32, name="w1w_raw", align_bytes=64)
+        w2s_raw = keep.tile([P, N], U8, name="w2s_raw", align_bytes=64)
+        w2w_raw = keep.tile([P, N], I32, name="w2w_raw", align_bytes=64)
+        gain = keep.tile([P, PACK], F32, name="gain")
+        page = [keep.tile([P, U], F32, name="page%d" % t) for t in range(PACK)]
+
+        nc.vector.memset(xs_all[:].bitcast(I32), 0)
+        nc.vector.memset(w1s_raw[:].bitcast(I32), 0)
+        nc.vector.memset(w2s_raw[:].bitcast(I32), 0)
+
+        nc.sync.dma_start(out=offs_t[:], in_=offs)
+        nc.sync.dma_start(out=w1w_raw[:], in_=as_words(w1_words))
+        load_scale_rows(xs_all, x_scales)
+        nc.sync.dma_start(out=xw_all[:], in_=as_words(x_words))
+        load_scale_rows(w1s_raw, w1_scales)
+        nc.sync.dma_start(out=n1_t[:], in_=n1)
+        nc.sync.dma_start(out=w2w_raw[:], in_=as_words(w2_words))
+        load_scale_rows(w2s_raw, w2_scales)
+        nc.sync.dma_start(out=gain[:], in_=gn.rearrange("(p t) o -> p (t o)", t=PACK))
+        nc.sync.dma_start(out=n2_t[:], in_=n2)
+        nc.sync.dma_start(out=n3_t[:], in_=n3)
+        mem_rows = mem.rearrange("(p t) w -> p t w", t=PACK)
+        for t in range(PACK):
+            nc.sync.dma_start(out=page[t][:], in_=mem_rows[:, t, :])
+
+        xs = keep.tile([P, S], U8, name="xs", tag="xs", align_bytes=64)
+        w1w = keep.tile([P, H], I32, name="w1w", tag="w1w", align_bytes=64)
+        w1s = keep.tile([P, H], U8, name="w1s", align_bytes=64)
+        deal(w1w, w1w_raw)
+        nc.vector.tensor_copy(out=xs[:], in_=xs_all[:].indirect(offs_t[:]))
+        xw = [keep.tile([P, HALF], U32, name="xw0", align_bytes=64)]
+
+        def pick_words(first, count):
+            nc.vector.tensor_copy(
+                out=xw[first // HALF][:, first % HALF : first % HALF + count],
+                in_=xw_all[:].bitcast(U32).indirect(entries(offs_t, first, count)),
+            )
+
+        pick_words(0, HALF)
+        deal(w1s, w1s_raw)
+        xw.append(keep.tile([P, HALF], U32, name="xw1", tag="w1s_raw", align_bytes=64))
+        pick_words(HALF, HALF // 2)
+        pick_words(HALF + HALF // 2, HALF // 2)
+        w2w = keep.tile([P, N], I32, name="w2w", align_bytes=64)
+        w2s = keep.tile([P, N], U8, name="w2s", align_bytes=64)
+        deal(w2w, w2w_raw)
+        deal(w2s, w2s_raw)
+
+        y = [keep.tile([P, S], F32, name="y%d" % t) for t in range(PACK)]
+        for t, first, count in (
+            (0, 0, 512), (1, 0, 512), (0, 512, 256), (0, 768, 256), (1, 512, 512),
+            (2, 0, 512), (2, 512, 512), (3, 0, 512), (3, 512, 512),
+        ):
+            acc = psum.tile([P, count], F32, name="acc")
+            cols = slice(first, first + count)
+            nc.tensor.matmul_mx(
+                out=acc[:],
+                lhsT=w1w[:, t * P : (t + 1) * P].bitcast(FP8X4),
+                lhsT_scale=w1s[:, t * P : (t + 1) * P],
+                rhs=xw[first // HALF][:, first % HALF : first % HALF + count].bitcast(FP8X4),
+                rhs_scale=xs[:, cols],
+                start=True,
+                stop=True,
+            )
+            nc.scalar.copy(out=y[t][:, cols], in_=acc[:])
+
+        z_codes = [keep.tile([P, PAIRS], U32, name="z_codes%d" % h, align_bytes=64) for h in range(2)]
+        z_scales = [keep.tile([P, PAIRS], U8, name="z_scales%d" % h, align_bytes=64) for h in range(2)]
+        z_packed = {}
+        planes = {}
+        accs = {}
+
+        def line_up(h, t, lined):
+            nc.vector.tensor_copy(
+                out=lined[:, t % 2 * HALF : (t % 2 + 1) * HALF], in_=y[t][:].indirect(entries(n1_t, h * HALF, HALF))
+            )
+
+        def make_z(h, u, lined, extremes):
+            pairs = lined[:].rearrange("p (v e) -> p v e", e=2)
+            larger, smaller = extremes[:, :HALF], extremes[:, HALF:]
+            spread = keep.tile([P, HALF], F32, name="spread%d%d" % (h, u))
+            nc.vector.tensor_tensor(out=larger, in0=pairs[:, :, 0], in1=pairs[:, :, 1], op=ALU.max)
+            nc.vector.tensor_tensor(out=smaller, in0=pairs[:, :, 0], in1=pairs[:, :, 1], op=ALU.min)
+            nc.vector.scalar_tensor_tensor(
+                out=spread[:], in0=smaller, scalar=-0.5, in1=larger, op0=ALU.mult, op1=ALU.add
+            )
+            for t in (2 * u, 2 * u + 1):
+                nc.scalar.activation(
+                    out=planes[h][:, t, :], in_=spread[:, t % 2 * PAIRS : (t % 2 + 1) * PAIRS], func=COPY, scale=gain[:, t : t + 1]
+                )
+
+        def pack_z(h):
+            z_packed[h] = keep.tile([P, PAIRS, PACK], BF16, name="z_packed%d" % h, tag="z_packed%d" % h, align_bytes=64)
+            nc.scalar.copy(out=z_packed[h][:], in_=planes[h][:].rearrange("p t v -> p v t"))
+
+        def second_product(h):
+            nc.vector.quantize_mx(
+                out=z_codes[h][:].bitcast(FP8X4), scales=z_scales[h][:], in_=z_packed[h][:].rearrange("p v t -> p (v t)")
+            )
+            for t in range(PACK):
+                acc = psum.tile([P, PAIRS], F32, name="acc")
+                nc.tensor.matmul_mx(
+                    out=acc[:],
+                    lhsT=w2w[:, t * P : (t + 1) * P].bitcast(FP8X4),
+                    lhsT_scale=w2s[:, t * P : (t + 1) * P],
+                    rhs=z_codes[h][:].bitcast(FP8X4),
+                    rhs_scale=z_scales[h][:],
+                    start=True,
+                    stop=True,
+                )
+                accs[h, t] = acc
+
+        def write_page(h, t, tag):
+            vals = keep.tile([P, PAIRS], F32, name="vals", tag=tag)
+            nc.scalar.copy(out=vals[:], in_=accs[h, t][:])
+            nc.vector.tensor_copy(out=page[t][:].indirect(entries(n2_t, h * PAIRS, PAIRS)), in_=vals[:])
+
+        def half_z(h, lined_tags, extremes_tags):
+            planes[h] = keep.tile([P, PACK, PAIRS], BF16, name="planes%d" % h, tag="planes%d" % h)
+            for u in range(2):
+                lined = keep.tile([P, 2 * HALF], F32, name="lined", tag=lined_tags[u], align_bytes=64)
+                extremes = keep.tile([P, 2 * HALF], F32, name="extremes", tag=extremes_tags[u], align_bytes=64)
+                line_up(h, 2 * u, lined)
+                line_up(h, 2 * u + 1, lined)
+                make_z(h, u, lined, extremes)
+            pack_z(h)
+
+        half_z(0, ("lined00", "lined01"), ("w1w", "extremes01"))
+        second_product(0)
+        half_z(1, ("w1w", "extremes01"), ("extremes10", "z_packed0"))
+        for t in range(PACK - 1):
+            write_page(0, t, "vals0%d" % t)
+        second_product(1)
+        write_page(0, PACK - 1, "planes1")
+        halved = [keep.tile([P, U], F32, name="halved%d" % t) for t in range(PACK)]
+        for t in range(PACK):
+            write_page(1, t, "vals1%d" % t)
+            nc.scalar.activation(out=halved[t][:], in_=page[t][:], func=COPY, scale=-0.5)
+
+        out_rows = out_0.rearrange("(p t) w -> p t w", t=PACK)
+        out_words = as_words(out_1)
+        o_codes = keep.tile([P, U], I32, name="o_codes", align_bytes=64)
+        o_scales = keep.tile([P, U], U8, name="o_scales", align_bytes=64)
+        chunks = U // OUT_CHUNK
+        o_packed = [keep.tile([P, OUT_CHUNK, PACK], BF16, name="o_packed%d" % c, align_bytes=64) for c in range(chunks)]
+
+        def result(c):
+            cols = slice(c * OUT_CHUNK, (c + 1) * OUT_CHUNK)
+            res = keep.tile([P, PACK, OUT_CHUNK], F32, name="res%d" % c)
+            for t in range(PACK):
+                nc.vector.tensor_tensor(
+                    out=res[:, t, :],
+                    in0=halved[t][:].indirect(entries(n3_t, c * OUT_CHUNK, OUT_CHUNK)),
+                    in1=page[t][:, cols],
+                    op=ALU.add,
+                )
+                if c == chunks - 1:
+                    nc.sync.dma_start(out=out_rows[:, t, cols], in_=res[:, t, :])
+            if c < chunks - 1:
+                nc.sync.dma_start(out=out_rows[:, :, cols], in_=res[:])
+                nc.scalar.copy(out=o_packed[c][:], in_=res[:].rearrange("p t w -> p w t"))
+            else:
+                nc.vector.tensor_copy(out=o_packed[c][:], in_=res[:].rearrange("p t w -> p w t"))
+
+        def hand_on(c):
+            cols = slice(c * OUT_CHUNK, (c + 1) * OUT_CHUNK)
+            nc.vector.quantize_mx(
+                out=o_codes[:, cols].bitcast(FP8X4), scales=o_scales[:, cols], in_=o_packed[c][:].rearrange("p w t -> p (w t)")
+            )
+            nc.sync.dma_start(out=out_words[:, cols], in_=o_codes[:, cols])
+
+        for c in range(chunks):
+            result(c)
+            if c > 0:
+                hand_on(c - 1)
+        hand_on(chunks - 1)
+        for q in range(4):
+            nc.scalar.dma_start(
+                out=out_2[0, 4 * q : 4 * q + 4, :].bitcast(I32), in_=o_scales[32 * q : 32 * q + 4, :].bitcast(I32)
+            )

@@ -1,6 +1,7 @@
 from contextlib import ExitStack
 
 import concourse.mybir as mybir
+from concourse.masks import make_identity
 
 K, T, S, V, N, H, U = 512, 2048, 1024, 512, 512, 512, 1024
 FLOPS = 2 * K * H * S + 2 * H * N * V
@@ -19,7 +20,8 @@ P = 128
 PACK = 4
 LANES = 16
 HALF = S // 2
-PAIRS = HALF // 2
+PAIRS = 128
+RELU = mybir.ActivationFunctionType.Relu
 OUT_CHUNK = 256
 
 
@@ -46,7 +48,11 @@ def tile_picked_laypgappagem_none_po_kernel(
     with ExitStack() as ctx:
         lists = ctx.enter_context(tc.tile_pool(name="lists", bufs=1))
         keep = ctx.enter_context(tc.tile_pool(name="keep", bufs=1))
-        psum = ctx.enter_context(tc.psum_pool(name="psum", bufs=8))
+        psum = ctx.enter_context(tc.psum_pool(name="psum", bufs=1))
+
+        def bank(b, cols):
+            return psum.tile([P, cols], F32, name="bank", tag="bank%d" % b)
+
 
         offs_t = lists.tile([P, S // LANES], U16, name="offs_t")
         n1_t = lists.tile([P, S // LANES], U16, name="n1_t")
@@ -62,9 +68,12 @@ def tile_picked_laypgappagem_none_po_kernel(
         gain = keep.tile([P, PACK], F32, name="gain")
         page = [keep.tile([P, U], F32, name="page%d" % t) for t in range(PACK)]
 
+        ident = keep.tile([P, P], F32, name="ident")
         nc.vector.memset(xs_all[:].bitcast(I32), 0)
         nc.vector.memset(w1s_raw[:].bitcast(I32), 0)
         nc.vector.memset(w2s_raw[:].bitcast(I32), 0)
+        nc.vector.memset(ident[:], 0.0)
+        make_identity(nc, ident[:], nomemset=True)
 
         nc.sync.dma_start(out=offs_t[:], in_=offs)
         nc.sync.dma_start(out=w1w_raw[:], in_=as_words(w1_words))
@@ -105,11 +114,11 @@ def tile_picked_laypgappagem_none_po_kernel(
         deal(w2s, w2s_raw)
 
         y = [keep.tile([P, S], F32, name="y%d" % t) for t in range(PACK)]
-        for t, first, count in (
+        for i, (t, first, count) in enumerate((
             (0, 0, 512), (1, 0, 512), (0, 512, 256), (0, 768, 256), (1, 512, 512),
             (2, 0, 512), (2, 512, 512), (3, 0, 512), (3, 512, 512),
-        ):
-            acc = psum.tile([P, count], F32, name="acc")
+        )):
+            acc = bank(i % 8, count)
             cols = slice(first, first + count)
             nc.tensor.matmul_mx(
                 out=acc[:],
@@ -122,116 +131,176 @@ def tile_picked_laypgappagem_none_po_kernel(
             )
             nc.scalar.copy(out=y[t][:, cols], in_=acc[:])
 
-        z_codes = [keep.tile([P, PAIRS], U32, name="z_codes%d" % h, align_bytes=64) for h in range(2)]
-        z_scales = [keep.tile([P, PAIRS], U8, name="z_scales%d" % h, align_bytes=64) for h in range(2)]
-        z_packed = {}
-        planes = {}
-        accs = {}
+        def slot(name, tag, cols, dtype=F32):
+            return keep.tile([P, cols], dtype, name=name, tag=tag, align_bytes=64)
 
-        def line_up(h, t, lined):
-            nc.vector.tensor_copy(
-                out=lined[:, t % 2 * HALF : (t % 2 + 1) * HALF], in_=y[t][:].indirect(entries(n1_t, h * HALF, HALF))
+        def by_tile(ap):
+            return ap.rearrange("p (t v) -> p t v", t=PACK)
+
+        def line_up(lined, first, count):
+            for t in range(PACK):
+                nc.vector.tensor_copy(
+                    out=lined[:, t * count : (t + 1) * count], in_=y[t][:].indirect(entries(n1_t, first, count))
+                )
+            return lined[:].rearrange("p (t v e) -> p t v e", t=PACK, e=2)
+
+        def round_z(c, spreads):
+            planes = slot("planes", "planes%d" % c, PACK * PAIRS, BF16)
+            for t in range(PACK):
+                nc.scalar.activation(
+                    out=planes[:, t * PAIRS : (t + 1) * PAIRS], in_=spreads[t], func=COPY, scale=gain[:, t : t + 1]
+                )
+            packed = slot("packed", "packed%d" % c, PACK * PAIRS, BF16)
+            nc.scalar.copy(
+                out=packed[:].rearrange("p (v t) -> p v t", t=PACK), in_=planes[:].rearrange("p (t v) -> p v t", t=PACK)
             )
+            return packed
 
-        def make_z(h, u, lined, extremes):
-            pairs = lined[:].rearrange("p (v e) -> p v e", e=2)
-            larger, smaller = extremes[:, :HALF], extremes[:, HALF:]
-            spread = keep.tile([P, HALF], F32, name="spread%d%d" % (h, u))
-            nc.vector.tensor_tensor(out=larger, in0=pairs[:, :, 0], in1=pairs[:, :, 1], op=ALU.max)
-            nc.vector.tensor_tensor(out=smaller, in0=pairs[:, :, 0], in1=pairs[:, :, 1], op=ALU.min)
+        def spread_on_vector(even, odd):
+            extremes = slot("extremes", "extremes", 2 * PACK * PAIRS)
+            larger, smaller = extremes[:, : PACK * PAIRS], extremes[:, PACK * PAIRS :]
+            spread = slot("spread", "spread", PACK * PAIRS)
+            nc.vector.tensor_tensor(out=by_tile(larger), in0=even, in1=odd, op=ALU.max)
+            nc.vector.tensor_tensor(out=by_tile(smaller), in0=even, in1=odd, op=ALU.min)
             nc.vector.scalar_tensor_tensor(
                 out=spread[:], in0=smaller, scalar=-0.5, in1=larger, op0=ALU.mult, op1=ALU.add
             )
-            for t in (2 * u, 2 * u + 1):
-                nc.scalar.activation(
-                    out=planes[h][:, t, :], in_=spread[:, t % 2 * PAIRS : (t % 2 + 1) * PAIRS], func=COPY, scale=gain[:, t : t + 1]
-                )
+            return [spread[:, t * PAIRS : (t + 1) * PAIRS] for t in range(PACK)]
 
-        def pack_z(h):
-            z_packed[h] = keep.tile([P, PAIRS, PACK], BF16, name="z_packed%d" % h, tag="z_packed%d" % h, align_bytes=64)
-            nc.scalar.copy(out=z_packed[h][:], in_=planes[h][:].rearrange("p t v -> p v t"))
-
-        def second_product(h):
-            nc.vector.quantize_mx(
-                out=z_codes[h][:].bitcast(FP8X4), scales=z_scales[h][:], in_=z_packed[h][:].rearrange("p v t -> p (v t)")
-            )
-            for t in range(PACK):
-                acc = psum.tile([P, PAIRS], F32, name="acc")
-                nc.tensor.matmul_mx(
-                    out=acc[:],
-                    lhsT=w2w[:, t * P : (t + 1) * P].bitcast(FP8X4),
-                    lhsT_scale=w2s[:, t * P : (t + 1) * P],
-                    rhs=z_codes[h][:].bitcast(FP8X4),
-                    rhs_scale=z_scales[h][:],
-                    start=True,
-                    stop=True,
-                )
-                accs[h, t] = acc
-
-        def write_page(h, t, tag):
-            vals = keep.tile([P, PAIRS], F32, name="vals", tag=tag)
-            nc.scalar.copy(out=vals[:], in_=accs[h, t][:])
-            nc.vector.tensor_copy(out=page[t][:].indirect(entries(n2_t, h * PAIRS, PAIRS)), in_=vals[:])
-
-        def half_z(h, lined_tags, extremes_tags):
-            planes[h] = keep.tile([P, PACK, PAIRS], BF16, name="planes%d" % h, tag="planes%d" % h)
+        def spread_on_tensor(c, even, odd, lift, sum_banks, back_banks):
+            diff = slot("diff", "diff%d" % c, PACK * PAIRS)
+            nc.vector.tensor_tensor(out=by_tile(diff[:]), in0=even, in1=odd, op=ALU.subtract)
+            turned = slot("turned", "turned%d" % c, PACK * P)
             for u in range(2):
-                lined = keep.tile([P, 2 * HALF], F32, name="lined", tag=lined_tags[u], align_bytes=64)
-                extremes = keep.tile([P, 2 * HALF], F32, name="extremes", tag=extremes_tags[u], align_bytes=64)
-                line_up(h, 2 * u, lined)
-                line_up(h, 2 * u + 1, lined)
-                make_z(h, u, lined, extremes)
-            pack_z(h)
+                two = slice(2 * u * P, 2 * (u + 1) * P)
+                nc.scalar.activation(out=lift[:, two], in_=diff[:, two], func=RELU, scale=-3.0)
+            for u in range(2):
+                summed = bank(sum_banks[u], 2 * P)
+                for t in (2 * u, 2 * u + 1):
+                    blk = slice(t * P, (t + 1) * P)
+                    terms = (lift[:, blk], even[:, t, :], diff[:, blk])
+                    for i, term in enumerate(terms):
+                        nc.tensor.matmul(
+                            out=summed[:, t % 2 * P : (t % 2 + 1) * P],
+                            lhsT=term,
+                            rhs=ident[:],
+                            start=(i == 0),
+                            stop=(i == len(terms) - 1),
+                            is_transpose=True,
+                        )
+                nc.scalar.activation(out=turned[:, 2 * u * P : 2 * (u + 1) * P], in_=summed[:], func=COPY, scale=0.5)
+            spreads = []
+            for u in range(2):
+                back = bank(back_banks[u], 2 * P)
+                for t in (2 * u, 2 * u + 1):
+                    part = back[:, t % 2 * P : (t % 2 + 1) * P]
+                    nc.tensor.transpose(out=part, in_=turned[:, t * P : (t + 1) * P], identity=ident[:])
+                    spreads.append(part)
+            return spreads
 
-        half_z(0, ("lined00", "lined01"), ("w1w", "extremes01"))
-        second_product(0)
-        half_z(1, ("w1w", "extremes01"), ("extremes10", "z_packed0"))
-        for t in range(PACK - 1):
-            write_page(0, t, "vals0%d" % t)
-        second_product(1)
-        write_page(0, PACK - 1, "planes1")
+        def second_product(c, packed, banks):
+            codes = slot("codes", "codes%d" % c, PAIRS, U32)
+            scales = slot("scales", "scales%d" % c, PAIRS, U8)
+            nc.vector.quantize_mx(out=codes[:].bitcast(FP8X4), scales=scales[:], in_=packed[:])
+            accs = []
+            for u in range(2):
+                acc = bank(banks[u], 2 * PAIRS)
+                for t in (2 * u, 2 * u + 1):
+                    nc.tensor.matmul_mx(
+                        out=acc[:, t % 2 * PAIRS : (t % 2 + 1) * PAIRS],
+                        lhsT=w2w[:, t * P : (t + 1) * P].bitcast(FP8X4),
+                        lhsT_scale=w2s[:, t * P : (t + 1) * P],
+                        rhs=codes[:].bitcast(FP8X4),
+                        rhs_scale=scales[:],
+                        start=True,
+                        stop=True,
+                    )
+                accs.append(acc)
+            return accs
+
         halved = [keep.tile([P, U], F32, name="halved%d" % t) for t in range(PACK)]
-        for t in range(PACK):
-            write_page(1, t, "vals1%d" % t)
-            nc.scalar.activation(out=halved[t][:], in_=page[t][:], func=COPY, scale=-0.5)
+
+        def write_page(c, u, acc, vals):
+            nc.scalar.copy(out=vals, in_=acc[:])
+            for t in (2 * u, 2 * u + 1):
+                nc.vector.tensor_copy(
+                    out=page[t][:].indirect(entries(n2_t, c * PAIRS, PAIRS)), in_=vals[:, t % 2 * PAIRS : (t % 2 + 1) * PAIRS]
+                )
+                if c == 3:
+                    nc.scalar.activation(out=halved[t][:], in_=page[t][:], func=COPY, scale=-0.5)
+
+        pairs01 = line_up(slot("lined", "lined01", PACK * HALF), 0, HALF)
+        packed0 = round_z(0, spread_on_vector(pairs01[:, :, :PAIRS, 0], pairs01[:, :, :PAIRS, 1]))
+        lift1 = slot("lift", "lift1", PACK * PAIRS)
+        back1 = spread_on_tensor(1, pairs01[:, :, PAIRS:, 0], pairs01[:, :, PAIRS:, 1], lift1[:], (0, 1), (2, 3))
+        pairs2 = line_up(slot("lined", "extremes", PACK * 2 * PAIRS), HALF, 2 * PAIRS)
+        packed1 = round_z(1, back1)
+        accs0 = second_product(0, packed0, (1, 3))
+        lift2 = slot("lift", "planes0", PACK * PAIRS)
+        back2 = spread_on_tensor(2, pairs2[:, :, :, 0], pairs2[:, :, :, 1], lift2[:], (4, 5), (6, 7))
+        pairs3 = line_up(slot("lined", "packed0", PACK * 2 * PAIRS), HALF + 2 * PAIRS, 2 * PAIRS)
+        write_page(0, 0, accs0[0], slot("vals", "vals0", 2 * PAIRS)[:])
+        packed2 = round_z(2, back2)
+        accs1 = second_product(1, packed1, (5, 7))
+        after1 = slot("after1", "planes1", (PACK + 2) * PAIRS)
+        write_page(0, 1, accs0[1], after1[:, PACK * PAIRS :])
+        back3 = spread_on_tensor(3, pairs3[:, :, :, 0], pairs3[:, :, :, 1], after1[:, : PACK * PAIRS], (0, 2), (4, 6))
+        write_page(1, 0, accs1[0], slot("vals", "vals1", 2 * PAIRS)[:])
+        packed3 = round_z(3, back3)
+        accs2 = second_product(2, packed2, (2, 6))
+        write_page(1, 1, accs1[1], slot("vals", "planes2", 2 * PAIRS)[:])
+        write_page(2, 0, accs2[0], slot("vals", "vals2", 2 * PAIRS)[:])
+        accs3 = second_product(3, packed3, (1, 3))
+        write_page(2, 1, accs2[1], slot("vals", "planes3", 2 * PAIRS)[:])
+        write_page(3, 0, accs3[0], slot("vals", "vals3", 2 * PAIRS)[:])
+        write_page(3, 1, accs3[1], slot("vals", "vals4", 2 * PAIRS)[:])
 
         out_rows = out_0.rearrange("(p t) w -> p t w", t=PACK)
         out_words = as_words(out_1)
         o_codes = keep.tile([P, U], I32, name="o_codes", align_bytes=64)
         o_scales = keep.tile([P, U], U8, name="o_scales", align_bytes=64)
-        chunks = U // OUT_CHUNK
-        o_packed = [keep.tile([P, OUT_CHUNK, PACK], BF16, name="o_packed%d" % c, align_bytes=64) for c in range(chunks)]
 
-        def result(c):
-            cols = slice(c * OUT_CHUNK, (c + 1) * OUT_CHUNK)
-            res = keep.tile([P, PACK, OUT_CHUNK], F32, name="res%d" % c)
+        def result(first, width, is_last):
+            cols = slice(first, first + width)
+            res = keep.tile([P, PACK, width], F32, name="res%d" % first)
+            o_packed = keep.tile([P, width, PACK], BF16, name="o_packed%d" % first, align_bytes=64)
             for t in range(PACK):
                 nc.vector.tensor_tensor(
                     out=res[:, t, :],
-                    in0=halved[t][:].indirect(entries(n3_t, c * OUT_CHUNK, OUT_CHUNK)),
+                    in0=halved[t][:].indirect(entries(n3_t, first, width)),
                     in1=page[t][:, cols],
                     op=ALU.add,
                 )
-                if c == chunks - 1:
-                    nc.sync.dma_start(out=out_rows[:, t, cols], in_=res[:, t, :])
-            if c < chunks - 1:
-                nc.sync.dma_start(out=out_rows[:, :, cols], in_=res[:])
-                nc.scalar.copy(out=o_packed[c][:], in_=res[:].rearrange("p t w -> p w t"))
+                if is_last and t % 2 == 1:
+                    nc.sync.dma_start(out=out_rows[:, t - 1 : t + 1, cols], in_=res[:, t - 1 : t + 1, :])
+                if is_last and t == 1:
+                    nc.scalar.copy(out=o_packed[:, :, :2], in_=res[:, :2, :].rearrange("p t w -> p w t"))
+            if is_last:
+                for w0 in range(0, width, P):
+                    nc.vector.tensor_copy(
+                        out=o_packed[:, w0 : w0 + P, 2:], in_=res[:, 2:, w0 : w0 + P].rearrange("p t w -> p w t")
+                    )
             else:
-                nc.vector.tensor_copy(out=o_packed[c][:], in_=res[:].rearrange("p t w -> p w t"))
+                nc.sync.dma_start(out=out_rows[:, :, cols], in_=res[:])
+                nc.scalar.copy(out=o_packed[:], in_=res[:].rearrange("p t w -> p w t"))
+            return o_packed
 
-        def hand_on(c):
-            cols = slice(c * OUT_CHUNK, (c + 1) * OUT_CHUNK)
-            nc.vector.quantize_mx(
-                out=o_codes[:, cols].bitcast(FP8X4), scales=o_scales[:, cols], in_=o_packed[c][:].rearrange("p w t -> p (w t)")
-            )
-            nc.sync.dma_start(out=out_words[:, cols], in_=o_codes[:, cols])
+        def hand_on(first, width, step, o_packed):
+            for w0 in range(0, width, step):
+                part = slice(first + w0, first + w0 + step)
+                nc.vector.quantize_mx(
+                    out=o_codes[:, part].bitcast(FP8X4),
+                    scales=o_scales[:, part],
+                    in_=o_packed[:, w0 : w0 + step, :].rearrange("p w t -> p (w t)"),
+                )
+            nc.sync.dma_start(out=out_words[:, first : first + width], in_=o_codes[:, first : first + width])
 
-        for c in range(chunks):
-            result(c)
-            if c > 0:
-                hand_on(c - 1)
-        hand_on(chunks - 1)
+        packed_a = result(0, 512, False)
+        packed_b = result(512, 256, False)
+        packed_c = result(768, 256, True)
+        hand_on(0, 512, 512, packed_a)
+        hand_on(512, 256, 256, packed_b)
+        hand_on(768, 256, 128, packed_c)
         for q in range(4):
             nc.scalar.dma_start(
                 out=out_2[0, 4 * q : 4 * q + 4, :].bitcast(I32), in_=o_scales[32 * q : 32 * q + 4, :].bitcast(I32)

@@ -15,14 +15,17 @@ U8 = mybir.dt.uint8
 FP8X4 = mybir.dt.float8_e4m3fn_x4
 ALU = mybir.AluOpType
 COPY = mybir.ActivationFunctionType.Copy
+RELU = mybir.ActivationFunctionType.Relu
 
 P = 128
 PACK = 4
 LANES = 16
+QUADRANTS = 4
+BANKS = 8
 HALF = S // 2
-PAIRS = 128
-RELU = mybir.ActivationFunctionType.Relu
-OUT_CHUNK = 256
+QUARTER = S // 4
+PAIRS = P
+LAST_CHUNK = V // PAIRS - 1
 
 
 def tile_picked_laypgappagem_none_po_kernel(
@@ -33,9 +36,13 @@ def tile_picked_laypgappagem_none_po_kernel(
     def as_words(words):
         return words[0].rearrange("p c r -> p (c r)").bitcast(I32)
 
-    def load_scale_rows(plane, scales):
-        for q in range(4):
-            nc.sync.dma_start(out=plane[32 * q : 32 * q + 4, :].bitcast(I32), in_=scales[0, 4 * q : 4 * q + 4, :].bitcast(I32))
+    def scale_rows(tile, scales, q):
+        return tile[32 * q : 32 * q + 4, :].bitcast(I32), scales[0, 4 * q : 4 * q + 4, :].bitcast(I32)
+
+    def load_scale_rows(tile, scales):
+        for q in range(QUADRANTS):
+            in_sbuf, in_hbm = scale_rows(tile, scales, q)
+            nc.sync.dma_start(out=in_sbuf, in_=in_hbm)
 
     def deal(dealt, raw):
         nc.vector.tensor_copy(
@@ -52,7 +59,6 @@ def tile_picked_laypgappagem_none_po_kernel(
 
         def bank(b, cols):
             return psum.tile([P, cols], F32, name="bank", tag="bank%d" % b)
-
 
         offs_t = lists.tile([P, S // LANES], U16, name="offs_t")
         n1_t = lists.tile([P, S // LANES], U16, name="n1_t")
@@ -90,8 +96,8 @@ def tile_picked_laypgappagem_none_po_kernel(
         for t in range(PACK):
             nc.sync.dma_start(out=page[t][:], in_=mem_rows[:, t, :])
 
-        xs = keep.tile([P, S], U8, name="xs", tag="xs", align_bytes=64)
-        w1w = keep.tile([P, H], I32, name="w1w", tag="w1w", align_bytes=64)
+        xs = keep.tile([P, S], U8, name="xs", align_bytes=64)
+        w1w = keep.tile([P, H], I32, name="w1w", align_bytes=64)
         w1s = keep.tile([P, H], U8, name="w1s", align_bytes=64)
         deal(w1w, w1w_raw)
         nc.vector.tensor_copy(out=xs[:], in_=xs_all[:].indirect(offs_t[:]))
@@ -106,19 +112,18 @@ def tile_picked_laypgappagem_none_po_kernel(
         pick_words(0, HALF)
         deal(w1s, w1s_raw)
         xw.append(keep.tile([P, HALF], U32, name="xw1", tag="w1s_raw", align_bytes=64))
-        pick_words(HALF, HALF // 2)
-        pick_words(HALF + HALF // 2, HALF // 2)
+        pick_words(HALF, QUARTER)
+        pick_words(HALF + QUARTER, QUARTER)
         w2w = keep.tile([P, N], I32, name="w2w", align_bytes=64)
         w2s = keep.tile([P, N], U8, name="w2s", align_bytes=64)
         deal(w2w, w2w_raw)
         deal(w2s, w2s_raw)
 
         y = [keep.tile([P, S], F32, name="y%d" % t) for t in range(PACK)]
-        for i, (t, first, count) in enumerate((
-            (0, 0, 512), (1, 0, 512), (0, 512, 256), (0, 768, 256), (1, 512, 512),
-            (2, 0, 512), (2, 512, 512), (3, 0, 512), (3, 512, 512),
-        )):
-            acc = bank(i % 8, count)
+        passes = [(0, 0, HALF), (1, 0, HALF), (0, HALF, QUARTER), (0, HALF + QUARTER, QUARTER), (1, HALF, HALF)]
+        passes.extend((t, first, HALF) for t in range(2, PACK) for first in (0, HALF))
+        for i, (t, first, count) in enumerate(passes):
+            acc = bank(i % BANKS, count)
             cols = slice(first, first + count)
             nc.tensor.matmul_mx(
                 out=acc[:],
@@ -131,10 +136,10 @@ def tile_picked_laypgappagem_none_po_kernel(
             )
             nc.scalar.copy(out=y[t][:, cols], in_=acc[:])
 
-        def slot(name, tag, cols, dtype=F32):
+        def buffer(name, tag, cols, dtype=F32):
             return keep.tile([P, cols], dtype, name=name, tag=tag, align_bytes=64)
 
-        def by_tile(ap):
+        def by_row_tile(ap):
             return ap.rearrange("p (t v) -> p t v", t=PACK)
 
         def line_up(lined, first, count):
@@ -145,35 +150,35 @@ def tile_picked_laypgappagem_none_po_kernel(
             return lined[:].rearrange("p (t v e) -> p t v e", t=PACK, e=2)
 
         def round_z(c, spreads):
-            planes = slot("planes", "planes%d" % c, PACK * PAIRS, BF16)
+            rounded = buffer("rounded", "rounded%d" % c, PACK * PAIRS, BF16)
             for t in range(PACK):
                 nc.scalar.activation(
-                    out=planes[:, t * PAIRS : (t + 1) * PAIRS], in_=spreads[t], func=COPY, scale=gain[:, t : t + 1]
+                    out=rounded[:, t * PAIRS : (t + 1) * PAIRS], in_=spreads[t], func=COPY, scale=gain[:, t : t + 1]
                 )
-            packed = slot("packed", "packed%d" % c, PACK * PAIRS, BF16)
+            woven = buffer("woven", "woven%d" % c, PACK * PAIRS, BF16)
             nc.scalar.copy(
-                out=packed[:].rearrange("p (v t) -> p v t", t=PACK), in_=planes[:].rearrange("p (t v) -> p v t", t=PACK)
+                out=woven[:].rearrange("p (v t) -> p v t", t=PACK), in_=rounded[:].rearrange("p (t v) -> p v t", t=PACK)
             )
-            return packed
+            return woven
 
         def spread_on_vector(even, odd):
-            extremes = slot("extremes", "extremes", 2 * PACK * PAIRS)
+            extremes = buffer("extremes", "extremes", 2 * PACK * PAIRS)
             larger, smaller = extremes[:, : PACK * PAIRS], extremes[:, PACK * PAIRS :]
-            spread = slot("spread", "spread", PACK * PAIRS)
-            nc.vector.tensor_tensor(out=by_tile(larger), in0=even, in1=odd, op=ALU.max)
-            nc.vector.tensor_tensor(out=by_tile(smaller), in0=even, in1=odd, op=ALU.min)
+            spread = buffer("spread", "spread", PACK * PAIRS)
+            nc.vector.tensor_tensor(out=by_row_tile(larger), in0=even, in1=odd, op=ALU.max)
+            nc.vector.tensor_tensor(out=by_row_tile(smaller), in0=even, in1=odd, op=ALU.min)
             nc.vector.scalar_tensor_tensor(
                 out=spread[:], in0=smaller, scalar=-0.5, in1=larger, op0=ALU.mult, op1=ALU.add
             )
             return [spread[:, t * PAIRS : (t + 1) * PAIRS] for t in range(PACK)]
 
         def spread_on_tensor(c, even, odd, lift, sum_banks, back_banks):
-            diff = slot("diff", "diff%d" % c, PACK * PAIRS)
-            nc.vector.tensor_tensor(out=by_tile(diff[:]), in0=even, in1=odd, op=ALU.subtract)
-            turned = slot("turned", "turned%d" % c, PACK * P)
+            diff = buffer("diff", "diff%d" % c, PACK * PAIRS)
+            nc.vector.tensor_tensor(out=by_row_tile(diff[:]), in0=even, in1=odd, op=ALU.subtract)
+            turned = buffer("turned", "turned%d" % c, PACK * P)
             for u in range(2):
-                two = slice(2 * u * P, 2 * (u + 1) * P)
-                nc.scalar.activation(out=lift[:, two], in_=diff[:, two], func=RELU, scale=-3.0)
+                both = slice(2 * u * P, 2 * (u + 1) * P)
+                nc.scalar.activation(out=lift[:, both], in_=diff[:, both], func=RELU, scale=-3.0)
             for u in range(2):
                 summed = bank(sum_banks[u], 2 * P)
                 for t in (2 * u, 2 * u + 1):
@@ -198,10 +203,10 @@ def tile_picked_laypgappagem_none_po_kernel(
                     spreads.append(part)
             return spreads
 
-        def second_product(c, packed, banks):
-            codes = slot("codes", "codes%d" % c, PAIRS, U32)
-            scales = slot("scales", "scales%d" % c, PAIRS, U8)
-            nc.vector.quantize_mx(out=codes[:].bitcast(FP8X4), scales=scales[:], in_=packed[:])
+        def second_product(c, woven, banks):
+            codes = buffer("codes", "codes%d" % c, PAIRS, U32)
+            scales = buffer("scales", "scales%d" % c, PAIRS, U8)
+            nc.vector.quantize_mx(out=codes[:].bitcast(FP8X4), scales=scales[:], in_=woven[:])
             accs = []
             for u in range(2):
                 acc = bank(banks[u], 2 * PAIRS)
@@ -226,34 +231,38 @@ def tile_picked_laypgappagem_none_po_kernel(
                 nc.vector.tensor_copy(
                     out=page[t][:].indirect(entries(n2_t, c * PAIRS, PAIRS)), in_=vals[:, t % 2 * PAIRS : (t % 2 + 1) * PAIRS]
                 )
-                if c == 3:
+                if c == LAST_CHUNK:
                     nc.scalar.activation(out=halved[t][:], in_=page[t][:], func=COPY, scale=-0.5)
 
-        pairs01 = line_up(slot("lined", "lined01", PACK * HALF), 0, HALF)
-        packed0 = round_z(0, spread_on_vector(pairs01[:, :, :PAIRS, 0], pairs01[:, :, :PAIRS, 1]))
-        lift1 = slot("lift", "lift1", PACK * PAIRS)
-        back1 = spread_on_tensor(1, pairs01[:, :, PAIRS:, 0], pairs01[:, :, PAIRS:, 1], lift1[:], (0, 1), (2, 3))
-        pairs2 = line_up(slot("lined", "extremes", PACK * 2 * PAIRS), HALF, 2 * PAIRS)
-        packed1 = round_z(1, back1)
-        accs0 = second_product(0, packed0, (1, 3))
-        lift2 = slot("lift", "planes0", PACK * PAIRS)
-        back2 = spread_on_tensor(2, pairs2[:, :, :, 0], pairs2[:, :, :, 1], lift2[:], (4, 5), (6, 7))
-        pairs3 = line_up(slot("lined", "packed0", PACK * 2 * PAIRS), HALF + 2 * PAIRS, 2 * PAIRS)
-        write_page(0, 0, accs0[0], slot("vals", "vals0", 2 * PAIRS)[:])
-        packed2 = round_z(2, back2)
-        accs1 = second_product(1, packed1, (5, 7))
-        after1 = slot("after1", "planes1", (PACK + 2) * PAIRS)
-        write_page(0, 1, accs0[1], after1[:, PACK * PAIRS :])
-        back3 = spread_on_tensor(3, pairs3[:, :, :, 0], pairs3[:, :, :, 1], after1[:, : PACK * PAIRS], (0, 2), (4, 6))
-        write_page(1, 0, accs1[0], slot("vals", "vals1", 2 * PAIRS)[:])
-        packed3 = round_z(3, back3)
-        accs2 = second_product(2, packed2, (2, 6))
-        write_page(1, 1, accs1[1], slot("vals", "planes2", 2 * PAIRS)[:])
-        write_page(2, 0, accs2[0], slot("vals", "vals2", 2 * PAIRS)[:])
-        accs3 = second_product(3, packed3, (1, 3))
-        write_page(2, 1, accs2[1], slot("vals", "planes3", 2 * PAIRS)[:])
-        write_page(3, 0, accs3[0], slot("vals", "vals3", 2 * PAIRS)[:])
-        write_page(3, 1, accs3[1], slot("vals", "vals4", 2 * PAIRS)[:])
+        lined_pair_cols = PACK * 2 * PAIRS
+        h_cols = 2 * PAIRS
+        pairs01 = line_up(buffer("lined", "lined01", PACK * HALF), 0, HALF)
+        woven0 = round_z(0, spread_on_vector(pairs01[:, :, :PAIRS, 0], pairs01[:, :, :PAIRS, 1]))
+        lift1 = buffer("lift", "lift1", PACK * PAIRS)
+        spreads1 = spread_on_tensor(1, pairs01[:, :, PAIRS:, 0], pairs01[:, :, PAIRS:, 1], lift1[:], (0, 1), (2, 3))
+        pairs2 = line_up(buffer("lined", "extremes", lined_pair_cols), HALF, QUARTER)
+        woven1 = round_z(1, spreads1)
+        h0 = second_product(0, woven0, (1, 3))
+        lift2 = buffer("lift", "rounded0", PACK * PAIRS)
+        spreads2 = spread_on_tensor(2, pairs2[:, :, :, 0], pairs2[:, :, :, 1], lift2[:], (4, 5), (6, 7))
+        pairs3 = line_up(buffer("lined", "woven0", lined_pair_cols), HALF + QUARTER, QUARTER)
+        write_page(0, 0, h0[0], buffer("vals", "vals0", h_cols)[:])
+        woven2 = round_z(2, spreads2)
+        h1 = second_product(1, woven1, (5, 7))
+        lift3_and_vals = buffer("lift3_and_vals", "rounded1", PACK * PAIRS + h_cols)
+        write_page(0, 1, h0[1], lift3_and_vals[:, PACK * PAIRS :])
+        spreads3 = spread_on_tensor(
+            3, pairs3[:, :, :, 0], pairs3[:, :, :, 1], lift3_and_vals[:, : PACK * PAIRS], (0, 2), (4, 6)
+        )
+        write_page(1, 0, h1[0], buffer("vals", "vals1", h_cols)[:])
+        woven3 = round_z(3, spreads3)
+        h2 = second_product(2, woven2, (0, 6))
+        write_page(1, 1, h1[1], buffer("vals", "rounded2", h_cols)[:])
+        write_page(2, 0, h2[0], buffer("vals", "vals2", h_cols)[:])
+        h3 = second_product(3, woven3, (1, 3))
+        write_page(2, 1, h2[1], buffer("vals", "rounded3", h_cols)[:])
+        write_page(3, 0, h3[0], buffer("vals", "vals3", h_cols)[:])
+        write_page(3, 1, h3[1], buffer("vals", "vals4", h_cols)[:])
 
         out_rows = out_0.rearrange("(p t) w -> p t w", t=PACK)
         out_words = as_words(out_1)
@@ -263,7 +272,7 @@ def tile_picked_laypgappagem_none_po_kernel(
         def result(first, width, is_last):
             cols = slice(first, first + width)
             res = keep.tile([P, PACK, width], F32, name="res%d" % first)
-            o_packed = keep.tile([P, width, PACK], BF16, name="o_packed%d" % first, align_bytes=64)
+            o_woven = keep.tile([P, width, PACK], BF16, name="o_woven%d" % first, align_bytes=64)
             for t in range(PACK):
                 nc.vector.tensor_tensor(
                     out=res[:, t, :],
@@ -274,34 +283,32 @@ def tile_picked_laypgappagem_none_po_kernel(
                 if is_last and t % 2 == 1:
                     nc.sync.dma_start(out=out_rows[:, t - 1 : t + 1, cols], in_=res[:, t - 1 : t + 1, :])
                 if is_last and t == 1:
-                    nc.scalar.copy(out=o_packed[:, :, :2], in_=res[:, :2, :].rearrange("p t w -> p w t"))
+                    nc.scalar.copy(out=o_woven[:, :, :2], in_=res[:, :2, :].rearrange("p t w -> p w t"))
             if is_last:
                 for w0 in range(0, width, P):
                     nc.vector.tensor_copy(
-                        out=o_packed[:, w0 : w0 + P, 2:], in_=res[:, 2:, w0 : w0 + P].rearrange("p t w -> p w t")
+                        out=o_woven[:, w0 : w0 + P, 2:], in_=res[:, 2:, w0 : w0 + P].rearrange("p t w -> p w t")
                     )
             else:
                 nc.sync.dma_start(out=out_rows[:, :, cols], in_=res[:])
-                nc.scalar.copy(out=o_packed[:], in_=res[:].rearrange("p t w -> p w t"))
-            return o_packed
+                nc.scalar.copy(out=o_woven[:], in_=res[:].rearrange("p t w -> p w t"))
+            return o_woven
 
-        def hand_on(first, width, step, o_packed):
+        def hand_on(first, width, step, o_woven):
             for w0 in range(0, width, step):
                 part = slice(first + w0, first + w0 + step)
                 nc.vector.quantize_mx(
                     out=o_codes[:, part].bitcast(FP8X4),
                     scales=o_scales[:, part],
-                    in_=o_packed[:, w0 : w0 + step, :].rearrange("p w t -> p (w t)"),
+                    in_=o_woven[:, w0 : w0 + step, :].rearrange("p w t -> p (w t)"),
                 )
             nc.sync.dma_start(out=out_words[:, first : first + width], in_=o_codes[:, first : first + width])
 
-        packed_a = result(0, 512, False)
-        packed_b = result(512, 256, False)
-        packed_c = result(768, 256, True)
-        hand_on(0, 512, 512, packed_a)
-        hand_on(512, 256, 256, packed_b)
-        hand_on(768, 256, 128, packed_c)
-        for q in range(4):
-            nc.scalar.dma_start(
-                out=out_2[0, 4 * q : 4 * q + 4, :].bitcast(I32), in_=o_scales[32 * q : 32 * q + 4, :].bitcast(I32)
-            )
+        pieces = ((0, U // 2, U // 2), (U // 2, U // 4, U // 4), (3 * U // 4, U // 4, P))
+        woven_pieces = [result(first, width, first + width == U) for first, width, step in pieces]
+        for (first, width, step), o_woven in zip(pieces, woven_pieces):
+            hand_on(first, width, step, o_woven)
+        for q in range(QUADRANTS):
+            in_sbuf, in_hbm = scale_rows(o_scales, out_2, q)
+            queue = nc.sync if q == QUADRANTS - 1 else nc.scalar
+            queue.dma_start(out=in_hbm, in_=in_sbuf)

from contextlib import ExitStack

import concourse.mybir as mybir
from concourse.masks import make_identity

K, T, S, V, N, H, U = 512, 2048, 1024, 512, 512, 512, 1024
FLOPS = 2 * K * H * S + 2 * H * N * V

F32 = mybir.dt.float32
BF16 = mybir.dt.bfloat16
I32 = mybir.dt.int32
U32 = mybir.dt.uint32
U16 = mybir.dt.uint16
U8 = mybir.dt.uint8
FP8X4 = mybir.dt.float8_e4m3fn_x4
ALU = mybir.AluOpType
COPY = mybir.ActivationFunctionType.Copy
RELU = mybir.ActivationFunctionType.Relu

P = 128
PACK = 4
LANES = 16
QUADRANTS = 4
BANKS = 8
HALF = S // 2
QUARTER = S // 4
PAIRS = P
LAST_CHUNK = V // PAIRS - 1


def tile_picked_laypgappagem_none_po_kernel(
    tc, x_words, x_scales, w1_words, w1_scales, gn, w2_words, w2_scales, mem, offs, n1, n2, n3, out_0, out_1, out_2
):
    nc = tc.nc

    def as_words(words):
        return words[0].rearrange("p c r -> p (c r)").bitcast(I32)

    def scale_rows(tile, scales, q):
        return tile[32 * q : 32 * q + 4, :].bitcast(I32), scales[0, 4 * q : 4 * q + 4, :].bitcast(I32)

    def load_scale_rows(tile, scales):
        for q in range(QUADRANTS):
            in_sbuf, in_hbm = scale_rows(tile, scales, q)
            nc.sync.dma_start(out=in_sbuf, in_=in_hbm)

    def deal(dealt, raw):
        nc.vector.tensor_copy(
            out=dealt[:].rearrange("p (t m) -> p m t", t=PACK), in_=raw[:].rearrange("p (m t) -> p m t", t=PACK)
        )

    def entries(list_tile, first, count):
        return list_tile[:, first // LANES : (first + count) // LANES]

    with ExitStack() as ctx:
        lists = ctx.enter_context(tc.tile_pool(name="lists", bufs=1))
        keep = ctx.enter_context(tc.tile_pool(name="keep", bufs=1))
        psum = ctx.enter_context(tc.psum_pool(name="psum", bufs=1))

        def bank(b, cols):
            return psum.tile([P, cols], F32, name="bank", tag="bank%d" % b)

        offs_t = lists.tile([P, S // LANES], U16, name="offs_t")
        n1_t = lists.tile([P, S // LANES], U16, name="n1_t")
        n2_t = lists.tile([P, V // LANES], U16, name="n2_t")
        n3_t = lists.tile([P, U // LANES], U16, name="n3_t")

        xs_all = keep.tile([P, T], U8, name="xs_all", align_bytes=64)
        xw_all = keep.tile([P, T], I32, name="xw_all", align_bytes=64)
        w1s_raw = keep.tile([P, H], U8, name="w1s_raw", tag="w1s_raw", align_bytes=64)
        w1w_raw = keep.tile([P, H], I32, name="w1w_raw", align_bytes=64)
        w2s_raw = keep.tile([P, N], U8, name="w2s_raw", align_bytes=64)
        w2w_raw = keep.tile([P, N], I32, name="w2w_raw", align_bytes=64)
        gain = keep.tile([P, PACK], F32, name="gain")
        page = [keep.tile([P, U], F32, name="page%d" % t) for t in range(PACK)]

        ident = keep.tile([P, P], F32, name="ident")
        nc.vector.memset(xs_all[:].bitcast(I32), 0)
        nc.vector.memset(w1s_raw[:].bitcast(I32), 0)
        nc.vector.memset(w2s_raw[:].bitcast(I32), 0)
        nc.vector.memset(ident[:], 0.0)
        make_identity(nc, ident[:], nomemset=True)

        nc.sync.dma_start(out=offs_t[:], in_=offs)
        nc.sync.dma_start(out=w1w_raw[:], in_=as_words(w1_words))
        load_scale_rows(xs_all, x_scales)
        nc.sync.dma_start(out=xw_all[:], in_=as_words(x_words))
        load_scale_rows(w1s_raw, w1_scales)
        nc.sync.dma_start(out=n1_t[:], in_=n1)
        nc.sync.dma_start(out=w2w_raw[:], in_=as_words(w2_words))
        load_scale_rows(w2s_raw, w2_scales)
        nc.sync.dma_start(out=gain[:], in_=gn.rearrange("(p t) o -> p (t o)", t=PACK))
        nc.sync.dma_start(out=n2_t[:], in_=n2)
        nc.sync.dma_start(out=n3_t[:], in_=n3)
        mem_rows = mem.rearrange("(p t) w -> p t w", t=PACK)
        for t in range(PACK):
            nc.sync.dma_start(out=page[t][:], in_=mem_rows[:, t, :])

        xs = keep.tile([P, S], U8, name="xs", align_bytes=64)
        w1w = keep.tile([P, H], I32, name="w1w", align_bytes=64)
        w1s = keep.tile([P, H], U8, name="w1s", align_bytes=64)
        deal(w1w, w1w_raw)
        nc.vector.tensor_copy(out=xs[:], in_=xs_all[:].indirect(offs_t[:]))
        xw = [keep.tile([P, HALF], U32, name="xw0", align_bytes=64)]

        def pick_words(first, count):
            nc.vector.tensor_copy(
                out=xw[first // HALF][:, first % HALF : first % HALF + count],
                in_=xw_all[:].bitcast(U32).indirect(entries(offs_t, first, count)),
            )

        pick_words(0, HALF)
        deal(w1s, w1s_raw)
        xw.append(keep.tile([P, HALF], U32, name="xw1", tag="w1s_raw", align_bytes=64))
        pick_words(HALF, QUARTER)
        pick_words(HALF + QUARTER, QUARTER)
        w2w = keep.tile([P, N], I32, name="w2w", align_bytes=64)
        w2s = keep.tile([P, N], U8, name="w2s", align_bytes=64)
        deal(w2w, w2w_raw)
        deal(w2s, w2s_raw)

        y = [keep.tile([P, S], F32, name="y%d" % t) for t in range(PACK)]
        passes = [(0, 0, HALF), (1, 0, HALF), (0, HALF, QUARTER), (0, HALF + QUARTER, QUARTER), (1, HALF, HALF)]
        passes.extend((t, first, HALF) for t in range(2, PACK) for first in (0, HALF))
        for i, (t, first, count) in enumerate(passes):
            acc = bank(i % BANKS, count)
            cols = slice(first, first + count)
            nc.tensor.matmul_mx(
                out=acc[:],
                lhsT=w1w[:, t * P : (t + 1) * P].bitcast(FP8X4),
                lhsT_scale=w1s[:, t * P : (t + 1) * P],
                rhs=xw[first // HALF][:, first % HALF : first % HALF + count].bitcast(FP8X4),
                rhs_scale=xs[:, cols],
                start=True,
                stop=True,
            )
            nc.scalar.copy(out=y[t][:, cols], in_=acc[:])

        def buffer(name, tag, cols, dtype=F32):
            return keep.tile([P, cols], dtype, name=name, tag=tag, align_bytes=64)

        def by_row_tile(ap):
            return ap.rearrange("p (t v) -> p t v", t=PACK)

        def line_up(lined, first, count):
            for t in range(PACK):
                nc.vector.tensor_copy(
                    out=lined[:, t * count : (t + 1) * count], in_=y[t][:].indirect(entries(n1_t, first, count))
                )
            return lined[:].rearrange("p (t v e) -> p t v e", t=PACK, e=2)

        def round_z(c, spreads):
            rounded = buffer("rounded", "rounded%d" % c, PACK * PAIRS, BF16)
            for t in range(PACK):
                nc.scalar.activation(
                    out=rounded[:, t * PAIRS : (t + 1) * PAIRS], in_=spreads[t], func=COPY, scale=gain[:, t : t + 1]
                )
            woven = buffer("woven", "woven%d" % c, PACK * PAIRS, BF16)
            nc.scalar.copy(
                out=woven[:].rearrange("p (v t) -> p v t", t=PACK), in_=rounded[:].rearrange("p (t v) -> p v t", t=PACK)
            )
            return woven

        def spread_on_vector(even, odd):
            extremes = buffer("extremes", "extremes", 2 * PACK * PAIRS)
            larger, smaller = extremes[:, : PACK * PAIRS], extremes[:, PACK * PAIRS :]
            spread = buffer("spread", "spread", PACK * PAIRS)
            nc.vector.tensor_tensor(out=by_row_tile(larger), in0=even, in1=odd, op=ALU.max)
            nc.vector.tensor_tensor(out=by_row_tile(smaller), in0=even, in1=odd, op=ALU.min)
            nc.vector.scalar_tensor_tensor(
                out=spread[:], in0=smaller, scalar=-0.5, in1=larger, op0=ALU.mult, op1=ALU.add
            )
            return [spread[:, t * PAIRS : (t + 1) * PAIRS] for t in range(PACK)]

        def spread_on_tensor(c, even, odd, lift, sum_banks, back_banks):
            diff = buffer("diff", "diff%d" % c, PACK * PAIRS)
            nc.vector.tensor_tensor(out=by_row_tile(diff[:]), in0=even, in1=odd, op=ALU.subtract)
            turned = buffer("turned", "turned%d" % c, PACK * P)
            for u in range(2):
                both = slice(2 * u * P, 2 * (u + 1) * P)
                nc.scalar.activation(out=lift[:, both], in_=diff[:, both], func=RELU, scale=-3.0)
            for u in range(2):
                summed = bank(sum_banks[u], 2 * P)
                for t in (2 * u, 2 * u + 1):
                    blk = slice(t * P, (t + 1) * P)
                    terms = (lift[:, blk], even[:, t, :], diff[:, blk])
                    for i, term in enumerate(terms):
                        nc.tensor.matmul(
                            out=summed[:, t % 2 * P : (t % 2 + 1) * P],
                            lhsT=term,
                            rhs=ident[:],
                            start=(i == 0),
                            stop=(i == len(terms) - 1),
                            is_transpose=True,
                        )
                nc.scalar.activation(out=turned[:, 2 * u * P : 2 * (u + 1) * P], in_=summed[:], func=COPY, scale=0.5)
            spreads = []
            for u in range(2):
                back = bank(back_banks[u], 2 * P)
                for t in (2 * u, 2 * u + 1):
                    part = back[:, t % 2 * P : (t % 2 + 1) * P]
                    nc.tensor.transpose(out=part, in_=turned[:, t * P : (t + 1) * P], identity=ident[:])
                    spreads.append(part)
            return spreads

        def second_product(c, woven, banks):
            codes = buffer("codes", "codes%d" % c, PAIRS, U32)
            scales = buffer("scales", "scales%d" % c, PAIRS, U8)
            nc.vector.quantize_mx(out=codes[:].bitcast(FP8X4), scales=scales[:], in_=woven[:])
            accs = []
            for u in range(2):
                acc = bank(banks[u], 2 * PAIRS)
                for t in (2 * u, 2 * u + 1):
                    nc.tensor.matmul_mx(
                        out=acc[:, t % 2 * PAIRS : (t % 2 + 1) * PAIRS],
                        lhsT=w2w[:, t * P : (t + 1) * P].bitcast(FP8X4),
                        lhsT_scale=w2s[:, t * P : (t + 1) * P],
                        rhs=codes[:].bitcast(FP8X4),
                        rhs_scale=scales[:],
                        start=True,
                        stop=True,
                    )
                accs.append(acc)
            return accs

        halved = [keep.tile([P, U], F32, name="halved%d" % t) for t in range(PACK)]

        def write_page(c, u, acc, vals):
            nc.scalar.copy(out=vals, in_=acc[:])
            for t in (2 * u, 2 * u + 1):
                nc.vector.tensor_copy(
                    out=page[t][:].indirect(entries(n2_t, c * PAIRS, PAIRS)), in_=vals[:, t % 2 * PAIRS : (t % 2 + 1) * PAIRS]
                )
                if c == LAST_CHUNK:
                    nc.scalar.activation(out=halved[t][:], in_=page[t][:], func=COPY, scale=-0.5)

        lined_pair_cols = PACK * 2 * PAIRS
        h_cols = 2 * PAIRS
        pairs01 = line_up(buffer("lined", "lined01", PACK * HALF), 0, HALF)
        woven0 = round_z(0, spread_on_vector(pairs01[:, :, :PAIRS, 0], pairs01[:, :, :PAIRS, 1]))
        lift1 = buffer("lift", "lift1", PACK * PAIRS)
        spreads1 = spread_on_tensor(1, pairs01[:, :, PAIRS:, 0], pairs01[:, :, PAIRS:, 1], lift1[:], (0, 1), (2, 3))
        pairs2 = line_up(buffer("lined", "extremes", lined_pair_cols), HALF, QUARTER)
        woven1 = round_z(1, spreads1)
        h0 = second_product(0, woven0, (1, 3))
        lift2 = buffer("lift", "rounded0", PACK * PAIRS)
        spreads2 = spread_on_tensor(2, pairs2[:, :, :, 0], pairs2[:, :, :, 1], lift2[:], (4, 5), (6, 7))
        pairs3 = line_up(buffer("lined", "woven0", lined_pair_cols), HALF + QUARTER, QUARTER)
        write_page(0, 0, h0[0], buffer("vals", "vals0", h_cols)[:])
        woven2 = round_z(2, spreads2)
        h1 = second_product(1, woven1, (5, 7))
        lift3_and_vals = buffer("lift3_and_vals", "rounded1", PACK * PAIRS + h_cols)
        write_page(0, 1, h0[1], lift3_and_vals[:, PACK * PAIRS :])
        spreads3 = spread_on_tensor(
            3, pairs3[:, :, :, 0], pairs3[:, :, :, 1], lift3_and_vals[:, : PACK * PAIRS], (0, 2), (4, 6)
        )
        write_page(1, 0, h1[0], buffer("vals", "vals1", h_cols)[:])
        woven3 = round_z(3, spreads3)
        h2 = second_product(2, woven2, (0, 6))
        write_page(1, 1, h1[1], buffer("vals", "rounded2", h_cols)[:])
        write_page(2, 0, h2[0], buffer("vals", "vals2", h_cols)[:])
        h3 = second_product(3, woven3, (1, 3))
        write_page(2, 1, h2[1], buffer("vals", "rounded3", h_cols)[:])
        write_page(3, 0, h3[0], buffer("vals", "vals3", h_cols)[:])
        write_page(3, 1, h3[1], buffer("vals", "vals4", h_cols)[:])

        out_rows = out_0.rearrange("(p t) w -> p t w", t=PACK)
        out_words = as_words(out_1)
        o_codes = keep.tile([P, U], I32, name="o_codes", align_bytes=64)
        o_scales = keep.tile([P, U], U8, name="o_scales", align_bytes=64)

        def result(first, width, is_last):
            cols = slice(first, first + width)
            res = keep.tile([P, PACK, width], F32, name="res%d" % first)
            o_woven = keep.tile([P, width, PACK], BF16, name="o_woven%d" % first, align_bytes=64)
            for t in range(PACK):
                nc.vector.tensor_tensor(
                    out=res[:, t, :],
                    in0=halved[t][:].indirect(entries(n3_t, first, width)),
                    in1=page[t][:, cols],
                    op=ALU.add,
                )
                if is_last and t % 2 == 1:
                    nc.sync.dma_start(out=out_rows[:, t - 1 : t + 1, cols], in_=res[:, t - 1 : t + 1, :])
                if is_last and t == 1:
                    nc.scalar.copy(out=o_woven[:, :, :2], in_=res[:, :2, :].rearrange("p t w -> p w t"))
            if is_last:
                for w0 in range(0, width, P):
                    nc.vector.tensor_copy(
                        out=o_woven[:, w0 : w0 + P, 2:], in_=res[:, 2:, w0 : w0 + P].rearrange("p t w -> p w t")
                    )
            else:
                nc.sync.dma_start(out=out_rows[:, :, cols], in_=res[:])
                nc.scalar.copy(out=o_woven[:], in_=res[:].rearrange("p t w -> p w t"))
            return o_woven

        def hand_on(first, width, step, o_woven):
            for w0 in range(0, width, step):
                part = slice(first + w0, first + w0 + step)
                nc.vector.quantize_mx(
                    out=o_codes[:, part].bitcast(FP8X4),
                    scales=o_scales[:, part],
                    in_=o_woven[:, w0 : w0 + step, :].rearrange("p w t -> p (w t)"),
                )
            nc.sync.dma_start(out=out_words[:, first : first + width], in_=o_codes[:, first : first + width])

        pieces = ((0, U // 2, U // 2), (U // 2, U // 4, U // 4), (3 * U // 4, U // 4, P))
        woven_pieces = [result(first, width, first + width == U) for first, width, step in pieces]
        for (first, width, step), o_woven in zip(pieces, woven_pieces):
            hand_on(first, width, step, o_woven)
        for q in range(QUADRANTS):
            in_sbuf, in_hbm = scale_rows(o_scales, out_2, q)
            queue = nc.sync if q == QUADRANTS - 1 else nc.scalar
            queue.dma_start(out=in_hbm, in_=in_sbuf)
